import numpy as np
import ml_dtypes


def mxq(x, axis, fmt="e4m3"):
    dtype, down = {"e4m3": (ml_dtypes.float8_e4m3fn, 7), "e5m2": (ml_dtypes.float8_e5m2, 14)}[fmt]
    v = np.moveaxis(np.asarray(x, np.float32).astype(ml_dtypes.bfloat16).astype(np.float64), axis, -1)
    blocks = v.reshape(v.shape[:-1] + (-1, 32))
    amax = np.abs(blocks).max(-1, keepdims=True)
    byte = np.maximum(np.where(amax > 0, np.frexp(amax)[1] - 1 + 127, 0) - down, 1)
    scale = np.exp2(byte - 127.0)
    codes = (blocks / scale).astype(np.float32).astype(dtype).astype(np.float64)
    return np.moveaxis((codes * scale).reshape(v.shape), -1, axis)


WIDE = False


def mx_kscale(k):
    if not WIDE:
        return np.ones(k)
    levels = np.array([30, -30])
    if k % 512:
        return np.exp2(np.random.permutation(np.resize(levels, k // 32))).repeat(32)
    a = np.empty((k // 512, 16))
    for p in range(k // 512):
        a[p, :8] = np.random.permutation(np.resize(levels, 8))
        for g in range(8):
            far = levels[np.abs(levels - a[p, g]) >= 10]
            a[p, g + 8] = far[np.random.randint(len(far))]
    return np.exp2(a.ravel()).repeat(32)


def f64(x):
    return np.asarray(x).astype(np.float64)


def striped(idx):
    return np.tile(np.asarray(idx).reshape(-1, 16).T, (8, 1)).astype(np.uint16)


def unstriped(offs):
    return offs[:16].T.reshape(-1).astype(np.int64)


E2M1 = np.array([0.0, 0.5, 1.0, 1.5, 2.0, 3.0, 4.0, 6.0, -0.0, -0.5, -1.0, -1.5, -2.0, -3.0, -4.0, -6.0])


def pack_weight(w, fmt):
    k, n = w.shape
    w = f64(np.asarray(w, np.float32).astype(ml_dtypes.bfloat16)).reshape(k // 32, 32, n)
    amax = np.abs(w).max(1)
    if fmt in ("e4m3", "e5m2"):
        byte = np.frexp(amax)[1] - 1 + 127 - (7 if fmt == "e4m3" else 14)
    else:
        mant, ex = np.frexp(amax / 6.0)
        byte = np.where(mant > 0.5, ex, ex - 1) + 127
    byte = np.clip(np.where(amax > 0, byte, 1), 1, 254)
    scaled = (w * np.exp2(127.0 - byte)[:, None, :]).reshape(k, n).astype(np.float32)
    by_word = np.ascontiguousarray(scaled.reshape(k // 512, 128, 4, n).transpose(0, 1, 3, 2))
    if fmt in ("e4m3", "e5m2"):
        words = by_word.astype(ml_dtypes.float8_e4m3fn if fmt == "e4m3" else ml_dtypes.float8_e5m2).view(np.uint8)
    else:
        c = by_word.astype(ml_dtypes.float4_e2m1fn).view(np.uint8) & 0xF
        words = (c[..., 0::2] | (c[..., 1::2] << 4)).reshape(k // 512, 128, 2 * n)
    return np.ascontiguousarray(words), np.ascontiguousarray(byte.astype(np.uint8).reshape(k // 512, 16, n))


def unpack_weight(words, scales, fmt):
    g, _, n = scales.shape
    words = np.ascontiguousarray(words).reshape(g, 128, n, -1)
    if fmt in ("e4m3", "e5m2"):
        vals = words.view(ml_dtypes.float8_e4m3fn if fmt == "e4m3" else ml_dtypes.float8_e5m2).astype(np.float64)
    else:
        nib = np.empty((g, 128, n, 4), np.uint8)
        nib[..., 0::2] = words & 0xF
        nib[..., 1::2] = words >> 4
        vals = E2M1[nib]
    vals = vals * np.repeat(np.exp2(scales.astype(np.float64) - 127.0), 8, axis=1)[..., None]
    return vals.transpose(0, 1, 3, 2).reshape(g * 512, n)


K, T, J, R, O, N = 512, 1024, 256, 512, 256, 256


def setup_inputs():
    n = np.random.standard_normal
    idx = np.random.permutation(T)[:J]
    idx2 = np.random.permutation(J)[:O]
    idx3 = np.random.permutation(J)[:O]
    idx4 = np.random.permutation(O)[:O]
    idx5 = np.random.permutation(T)[:O]
    fk = mx_kscale(K)
    fr = mx_kscale(R)
    xtp = pack_weight(n((K, T)) / fk[:, None], "e4m3")
    wp = pack_weight(n((K, R)) * 1 / np.sqrt(K) * fk[:, None] * fr, "e2m1")
    w2p = pack_weight(n((K, R)) * 1 / np.sqrt(K) * fk[:, None] * fr, "e5m2")
    wbp = pack_weight(n((R, N)) * 1 / np.sqrt(R) / fr[:, None], "e5m2")
    wsp = pack_weight(n((K, N)) * 1 / np.sqrt(K) * fk[:, None], "e5m2")
    return {
        "xt_words": xtp[0],
        "xt_scales": xtp[1],
        "w_words": wp[0],
        "w_scales": wp[1],
        "w2_words": w2p[0],
        "w2_scales": w2p[1],
        "wb_words": wbp[0],
        "wb_scales": wbp[1],
        "ws_words": wsp[0],
        "ws_scales": wsp[1],
        "offs": striped(idx),
        "offs2": striped(idx2),
        "offs3": striped(idx3),
        "offs4": striped(idx4),
        "offs5": striped(idx5),
    }


def reference(xt_words, xt_scales, w_words, w_scales, w2_words, w2_scales, wb_words, wb_scales, ws_words, ws_scales, offs, offs2, offs3, offs4, offs5):
    idx = unstriped(offs)
    idx2 = unstriped(offs2)
    idx3 = unstriped(offs3)
    idx4 = unstriped(offs4)
    idx5 = unstriped(offs5)
    xtu = unpack_weight(xt_words, xt_scales, "e4m3")
    wu = unpack_weight(w_words, w_scales, "e2m1")
    w2u = unpack_weight(w2_words, w2_scales, "e5m2")
    wbu = unpack_weight(wb_words, wb_scales, "e5m2")
    wsu = unpack_weight(ws_words, ws_scales, "e5m2")
    xtidxg = xtu[:, idx]
    a = wu.T @ xtidxg
    b = w2u.T @ xtidxg
    ca = np.maximum(a[:, idx2], b[:, idx3])
    hid = np.abs(ca - ca[:, idx4])
    hidq = mxq(hid, 0, "e4m3")
    xtidx5g = xtu[:, idx5]
    y = wbu.T @ hidq + wsu.T @ xtidx5g
    return y

@@ -1,0 +1,222 @@
+from contextlib import ExitStack
+
+import concourse.mybir as mybir
+
+K, T, J, R, O, N = 512, 1024, 256, 512, 256, 256
+FLOPS = 2 * (2 * K * R * J + R * N * O + K * N * O)
+
+F32 = mybir.dt.float32
+BF16 = mybir.dt.bfloat16
+I32 = mybir.dt.int32
+U32 = mybir.dt.uint32
+U16 = mybir.dt.uint16
+U8 = mybir.dt.uint8
+E4M3 = mybir.dt.float8_e4m3fn_x4
+E5M2 = mybir.dt.float8_e5m2_x4
+E2M1 = mybir.dt.float4_e2m1fn_x4
+ACT = mybir.ActivationFunctionType
+ALU = mybir.AluOpType
+
+P = 128
+PACK = 4
+HALF = O // 2
+LIST_COLS = J // 16
+
+
+def load_scale_rows(queue, plane, scales, quadrants):
+    for q in quadrants:
+        queue.dma_start(out=plane[32 * q : 32 * q + 4, :].bitcast(I32), in_=scales[0, 4 * q : 4 * q + 4, :].bitcast(I32))
+
+
+def load_scale_rows_filled(queue, plane, scales, quadrants):
+    width = scales.shape[2] // 4
+    for q in quadrants:
+        rows = scales[0, 4 * q : 4 * q + 4, :].bitcast(I32).rearrange("(o r) w -> o r w", o=1)
+        queue.dma_start(out=plane[32 * q : 32 * q + 32, :].bitcast(I32), in_=rows.to_broadcast([8, 4, width]))
+
+
+def tile_list_pairedplaces_twow_further_plain_kernel(
+    tc, xt_words, xt_scales, w_words, w_scales, w2_words, w2_scales, wb_words, wb_scales, ws_words, ws_scales,
+    offs, offs2, offs3, offs4, offs5, out,
+):
+    nc = tc.nc
+    with ExitStack() as ctx:
+        lists = ctx.enter_context(tc.tile_pool(name="lists", bufs=1))
+        keep = ctx.enter_context(tc.tile_pool(name="keep", bufs=1))
+        psum = ctx.enter_context(tc.psum_pool(name="psum", bufs=1))
+
+        idx = lists.tile([P, LIST_COLS], U16, name="idx")
+        idx2 = lists.tile([P, LIST_COLS], U16, name="idx2")
+        idx3 = lists.tile([P, LIST_COLS], U16, name="idx3")
+        idx4 = lists.tile([P, LIST_COLS], U16, name="idx4")
+        idx5 = lists.tile([P, LIST_COLS], U16, name="idx5")
+
+        xt_w = keep.tile([P, T], I32, name="xt_w", align_bytes=64)
+        xt_s = keep.tile([P, T], U8, name="xt_s", align_bytes=64)
+        w_raw = keep.tile([P, 2 * R], U8, name="w_raw", align_bytes=64)
+        w2_raw = keep.tile([P, R], I32, name="w2_raw", align_bytes=64)
+        w_s_raw = keep.tile([P, R], U8, name="w_s_raw", align_bytes=64)
+        w2_s_raw = keep.tile([P, R], U8, name="w2_s_raw", align_bytes=64)
+        wb_w = keep.tile([P, N], I32, name="wb_w", align_bytes=64)
+        ws_w = keep.tile([P, N], I32, name="ws_w", align_bytes=64)
+        wb_s = keep.tile([P, N], U8, name="wb_s", align_bytes=64)
+        ws_s = keep.tile([P, N], U8, name="ws_s", align_bytes=64)
+        a_sb = [keep.tile([P, 3 * J], F32, name="a_sb%d" % u) for u in range(2)]
+        b_sb = [keep.tile([P, 3 * J], F32, name="b_sb%d" % u) for u in range(2)]
+
+        for plane in (ws_s, wb_s):
+            nc.vector.memset(plane[:].bitcast(I32), 0)
+        for t in a_sb + b_sb:
+            nc.vector.memset(t[:, 2 * J :], 0.0)
+
+        nc.gpsimd.dma_start(out=w2_raw[:], in_=w2_words[0].rearrange("p c r -> p (c r)").bitcast(I32))
+        nc.sync.dma_start(idx[:], offs)
+        load_scale_rows_filled(nc.sync, xt_s, xt_scales, range(4))
+        load_scale_rows_filled(nc.sync, w_s_raw, w_scales, range(1))
+        nc.sync.dma_start(out=xt_w[:], in_=xt_words[0].rearrange("p c r -> p (c r)").bitcast(I32))
+        nc.sync.dma_start(out=w_raw[:].bitcast(I32), in_=w_words[0].bitcast(I32))
+        load_scale_rows_filled(nc.sync, w_s_raw, w_scales, range(1, 4))
+        nc.sync.dma_start(idx5[:], offs5)
+        load_scale_rows_filled(nc.sync, w2_s_raw, w2_scales, range(2))
+        nc.sync.dma_start(idx2[:], offs2)
+        load_scale_rows_filled(nc.sync, w2_s_raw, w2_scales, range(2, 4))
+        nc.sync.dma_start(idx3[:], offs3)
+        nc.sync.dma_start(idx4[:], offs4)
+        nc.sync.dma_start(out=ws_w[:], in_=ws_words[0].rearrange("p c r -> p (c r)").bitcast(I32))
+        load_scale_rows(nc.sync, ws_s, ws_scales, range(4))
+        nc.sync.dma_start(out=wb_w[:], in_=wb_words[0].rearrange("p c r -> p (c r)").bitcast(I32))
+        load_scale_rows(nc.sync, wb_s, wb_scales, range(4))
+
+        xg_s = keep.tile([P, J], U8, name="xg_s", align_bytes=64)
+        xg_w = keep.tile([P, J], U32, name="xg_w", align_bytes=64)
+        x5_s = keep.tile([P, O], U8, name="x5_s", align_bytes=64)
+        x5_w = keep.tile([P, O], U32, name="x5_w", align_bytes=64)
+        w_w = keep.tile([P, 2 * R], U8, name="w_w", align_bytes=64)
+        w2_w = keep.tile([P, R], U32, name="w2_w", align_bytes=64)
+        w_s = keep.tile([P, R], U8, name="w_s", align_bytes=64)
+        w2_s = keep.tile([P, R], U8, name="w2_s", align_bytes=64)
+        a_ps = [psum.tile([P, 2 * J], F32, name="a_ps%d" % u) for u in range(2)]
+        b_ps = [psum.tile([P, 2 * J], F32, name="b_ps%d" % u) for u in range(2)]
+        y_ps = [[psum.tile([P, HALF], F32, name="y_ps%d%d" % (h, g)) for g in range(2)] for h in range(2)]
+        a_g = [keep.tile([P, 2 * O], F32, name="a_g%d" % u) for u in range(2)]
+        b_g = [keep.tile([P, 2 * O], F32, name="b_g%d" % u) for u in range(2)]
+        ca = keep.tile([P, PACK * O], F32, name="ca")
+        c_g = [keep.tile([P, PACK * HALF], F32, name="c_g%d" % h) for h in range(2)]
+        diff = [keep.tile([P, PACK * HALF], F32, name="diff%d" % h) for h in range(2)]
+        hid = [keep.tile([P, HALF * PACK], BF16, name="hid%d" % h, align_bytes=64) for h in range(2)]
+        hq_w = [keep.tile([P, HALF], U32, name="hq_w%d" % h, align_bytes=64) for h in range(2)]
+        hq_s = [keep.tile([P, HALF], U8, name="hq_s%d" % h, align_bytes=64) for h in range(2)]
+        y_sb = [keep.tile([P, 2, HALF], F32, name="y_sb%d" % h) for h in range(2)]
+        out_v = out.rearrange("(g p) o -> p g o", p=P)
+
+        def on_vector(dst, src):
+            nc.vector.tensor_copy(dst, src)
+
+        def on_scalar(dst, src):
+            nc.scalar.activation(dst, src, ACT.Copy)
+
+        def deal(copy, dst, src):
+            copy(dst.rearrange("p (t m) -> p m t", t=PACK), src.rearrange("p (m t) -> p m t", t=PACK))
+
+        def first_stage(ps, words, width, scales, fmt):
+            for t in range(PACK):
+                nc.tensor.matmul_mx(
+                    out=ps[t // 2][:, (t % 2) * J : (t % 2 + 1) * J],
+                    lhsT=words[:, width * P * t : width * P * (t + 1)].bitcast(fmt), lhsT_scale=scales[:, P * t : P * (t + 1)],
+                    rhs=xg_w[:].bitcast(E4M3), rhs_scale=xg_s[:], start=True, stop=True,
+                )
+
+        def empty(copy, sb, ps, u):
+            copy(sb[u][:, : 2 * J], ps[u][:])
+
+        def look(copy, dst, sb, offsets, t):
+            u, v = divmod(t, 2)
+            copy(dst[u][:, v * O : (v + 1) * O], sb[u][:, v * J : (v + 2) * J].indirect(offsets[:]))
+
+        def larger(u):
+            nc.vector.tensor_tensor(ca[:, 2 * u * O : 2 * (u + 1) * O], a_g[u][:], b_g[u][:], ALU.max)
+
+        def neighbour(copy, t, h):
+            copy(c_g[h][:, t * HALF : (t + 1) * HALF], ca[:, t * O : (t + 1) * O].indirect(idx4[:, h * 8 : (h + 1) * 8]))
+
+        def subtract(h):
+            nc.vector.tensor_tensor(
+                diff[h][:].rearrange("p (t o) -> p t o", t=PACK),
+                ca[:].rearrange("p (t o) -> p t o", t=PACK)[:, :, h * HALF : (h + 1) * HALF],
+                c_g[h][:].rearrange("p (t o) -> p t o", t=PACK),
+                ALU.subtract,
+            )
+
+        def magnitude(h):
+            nc.scalar.activation(
+                hid[h][:].rearrange("p (c i t) -> p c t i", i=4, t=PACK),
+                diff[h][:].rearrange("p (t c i) -> p c t i", i=4, t=PACK),
+                ACT.Abs,
+            )
+
+        def quantise(h):
+            nc.vector.quantize_mx(out=hq_w[h][:].bitcast(E4M3), scales=hq_s[h][:], in_=hid[h][:])
+
+        def short_way(h, g):
+            rows, cols = slice(g * P, (g + 1) * P), slice(h * HALF, (h + 1) * HALF)
+            nc.tensor.matmul_mx(
+                out=y_ps[h][g][:], lhsT=ws_w[:, rows].bitcast(E5M2), lhsT_scale=ws_s[:, rows],
+                rhs=x5_w[:, cols].bitcast(E4M3), rhs_scale=x5_s[:, cols], start=True, stop=False,
+            )
+
+        def second_stage(h, g):
+            rows = slice(g * P, (g + 1) * P)
+            nc.tensor.matmul_mx(
+                out=y_ps[h][g][:], lhsT=wb_w[:, rows].bitcast(E5M2), lhsT_scale=wb_s[:, rows],
+                rhs=hq_w[h][:].bitcast(E4M3), rhs_scale=hq_s[h][:], start=False, stop=True,
+            )
+
+        def store(h):
+            nc.sync.dma_start(out=out_v[:, :, h * HALF : (h + 1) * HALF], in_=y_sb[h][:])
+
+        on_vector(xg_s[:], xt_s[:].indirect(idx[:]))
+        on_vector(xg_w[:], xt_w[:].bitcast(U32).indirect(idx[:]))
+        deal(nc.scalar.copy, w_w[:].bitcast(U16), w_raw[:].bitcast(U16))
+        deal(on_vector, w_s[:], w_s_raw[:])
+        deal(nc.scalar.copy, w2_w[:], w2_raw[:].bitcast(U32))
+        first_stage(a_ps, w_w, 2, w_s, E2M1)
+        on_vector(x5_s[:], xt_s[:].indirect(idx5[:]))
+        on_vector(x5_w[:], xt_w[:].bitcast(U32).indirect(idx5[:]))
+        empty(on_vector, a_sb, a_ps, 0)
+        empty(nc.scalar.copy, a_sb, a_ps, 1)
+        deal(on_vector, w2_s[:], w2_s_raw[:])
+        first_stage(b_ps, w2_w, 1, w2_s, E5M2)
+        look(on_vector, a_g, a_sb, idx2, 0)
+        for t in (2, 3, 1):
+            look(on_scalar, a_g, a_sb, idx2, t)
+        empty(on_vector, b_sb, b_ps, 0)
+        empty(nc.scalar.copy, b_sb, b_ps, 1)
+        for h in range(2):
+            for g in range(2):
+                short_way(h, g)
+        look(on_vector, b_g, b_sb, idx3, 0)
+        look(on_vector, b_g, b_sb, idx3, 1)
+        look(on_scalar, b_g, b_sb, idx3, 2)
+        look(on_scalar, b_g, b_sb, idx3, 3)
+        larger(0)
+        larger(1)
+        neighbour(on_scalar, 0, 0)
+        neighbour(on_scalar, 1, 0)
+        neighbour(on_vector, 2, 0)
+        neighbour(on_scalar, 3, 0)
+        subtract(0)
+        neighbour(on_scalar, 0, 1)
+        neighbour(on_scalar, 1, 1)
+        neighbour(on_vector, 2, 1)
+        neighbour(on_scalar, 3, 1)
+        magnitude(0)
+        subtract(1)
+        magnitude(1)
+        for h in range(2):
+            quantise(h)
+            for g in range(2):
+                second_stage(h, g)
+        for h in range(2):
+            on_vector(y_sb[h][:, 0, :], y_ps[h][0][:])
+            nc.scalar.copy(y_sb[h][:, 1, :], y_ps[h][1][:])
+            store(h)

@@ -21,6 +21,7 @@ P = 128
 PACK = 4
 HALF = O // 2
 LIST_COLS = J // 16
+WINDOW = 352
 
 
 def load_scale_rows(queue, plane, scales, quadrants):
@@ -55,31 +56,30 @@ def tile_list_pairedplaces_twow_further_plain_kernel(
         xt_s = keep.tile([P, T], U8, name="xt_s", align_bytes=64)
         w_raw = keep.tile([P, 2 * R], U8, name="w_raw", align_bytes=64)
         w2_raw = keep.tile([P, R], I32, name="w2_raw", align_bytes=64)
-        w_s_raw = keep.tile([P, R], U8, name="w_s_raw", align_bytes=64)
+        w_s_raw = keep.tile([P, R], U8, name="w_s_raw", tag="w_s_then_x5", align_bytes=64)
         w2_s_raw = keep.tile([P, R], U8, name="w2_s_raw", align_bytes=64)
         wb_w = keep.tile([P, N], I32, name="wb_w", align_bytes=64)
         ws_w = keep.tile([P, N], I32, name="ws_w", align_bytes=64)
         wb_s = keep.tile([P, N], U8, name="wb_s", align_bytes=64)
         ws_s = keep.tile([P, N], U8, name="ws_s", align_bytes=64)
-        a_sb = [keep.tile([P, 3 * J], F32, name="a_sb%d" % u) for u in range(2)]
-        b_sb = [keep.tile([P, 3 * J], F32, name="b_sb%d" % u) for u in range(2)]
+        a_sb = [keep.tile([P, WINDOW], F32, name="a_sb%d" % t) for t in range(PACK)]
+        b_sb = [keep.tile([P, WINDOW], F32, name="b_sb%d" % t) for t in range(PACK)]
 
         for plane in (ws_s, wb_s):
             nc.vector.memset(plane[:].bitcast(I32), 0)
         for t in a_sb + b_sb:
-            nc.vector.memset(t[:, 2 * J :], 0.0)
+            nc.vector.memset(t[:, J:], 0.0)
 
         nc.gpsimd.dma_start(out=w2_raw[:], in_=w2_words[0].rearrange("p c r -> p (c r)").bitcast(I32))
+        load_scale_rows_filled(nc.gpsimd, w2_s_raw, w2_scales, range(2, 4))
         nc.sync.dma_start(idx[:], offs)
         load_scale_rows_filled(nc.sync, xt_s, xt_scales, range(4))
-        load_scale_rows_filled(nc.sync, w_s_raw, w_scales, range(1))
         nc.sync.dma_start(out=xt_w[:], in_=xt_words[0].rearrange("p c r -> p (c r)").bitcast(I32))
         nc.sync.dma_start(out=w_raw[:].bitcast(I32), in_=w_words[0].bitcast(I32))
-        load_scale_rows_filled(nc.sync, w_s_raw, w_scales, range(1, 4))
         nc.sync.dma_start(idx5[:], offs5)
+        load_scale_rows_filled(nc.sync, w_s_raw, w_scales, range(4))
         load_scale_rows_filled(nc.sync, w2_s_raw, w2_scales, range(2))
         nc.sync.dma_start(idx2[:], offs2)
-        load_scale_rows_filled(nc.sync, w2_s_raw, w2_scales, range(2, 4))
         nc.sync.dma_start(idx3[:], offs3)
         nc.sync.dma_start(idx4[:], offs4)
         nc.sync.dma_start(out=ws_w[:], in_=ws_words[0].rearrange("p c r -> p (c r)").bitcast(I32))
@@ -90,16 +90,15 @@ def tile_list_pairedplaces_twow_further_plain_kernel(
         xg_s = keep.tile([P, J], U8, name="xg_s", align_bytes=64)
         xg_w = keep.tile([P, J], U32, name="xg_w", align_bytes=64)
         x5_s = keep.tile([P, O], U8, name="x5_s", align_bytes=64)
-        x5_w = keep.tile([P, O], U32, name="x5_w", align_bytes=64)
         w_w = keep.tile([P, 2 * R], U8, name="w_w", align_bytes=64)
         w2_w = keep.tile([P, R], U32, name="w2_w", align_bytes=64)
         w_s = keep.tile([P, R], U8, name="w_s", align_bytes=64)
         w2_s = keep.tile([P, R], U8, name="w2_s", align_bytes=64)
-        a_ps = [psum.tile([P, 2 * J], F32, name="a_ps%d" % u) for u in range(2)]
-        b_ps = [psum.tile([P, 2 * J], F32, name="b_ps%d" % u) for u in range(2)]
-        y_ps = [[psum.tile([P, HALF], F32, name="y_ps%d%d" % (h, g)) for g in range(2)] for h in range(2)]
-        a_g = [keep.tile([P, 2 * O], F32, name="a_g%d" % u) for u in range(2)]
-        b_g = [keep.tile([P, 2 * O], F32, name="b_g%d" % u) for u in range(2)]
+        a_ps = [psum.tile([P, J], F32, name="a_ps%d" % t) for t in range(PACK)]
+        b_ps = [psum.tile([P, J], F32, name="b_ps%d" % t, tag="bank_b%d" % t) for t in range(PACK)]
+        y_ps = {}
+        a_g = keep.tile([P, PACK * O], F32, name="a_g")
+        b_g = keep.tile([P, PACK * O], F32, name="b_g")
         ca = keep.tile([P, PACK * O], F32, name="ca")
         c_g = [keep.tile([P, PACK * HALF], F32, name="c_g%d" % h) for h in range(2)]
         diff = [keep.tile([P, PACK * HALF], F32, name="diff%d" % h) for h in range(2)]
@@ -115,35 +114,35 @@ def tile_list_pairedplaces_twow_further_plain_kernel(
         def on_scalar(dst, src):
             nc.scalar.activation(dst, src, ACT.Copy)
 
-        def deal(copy, dst, src):
-            copy(dst.rearrange("p (t m) -> p m t", t=PACK), src.rearrange("p (m t) -> p m t", t=PACK))
+        def deal(copy, dst, src, t0=0, t1=PACK):
+            copy(dst.rearrange("p (t m) -> p m t", t=PACK)[:, :, t0:t1], src.rearrange("p (m t) -> p m t", t=PACK)[:, :, t0:t1])
 
         def first_stage(ps, words, width, scales, fmt):
             for t in range(PACK):
                 nc.tensor.matmul_mx(
-                    out=ps[t // 2][:, (t % 2) * J : (t % 2 + 1) * J],
+                    out=ps[t][:],
                     lhsT=words[:, width * P * t : width * P * (t + 1)].bitcast(fmt), lhsT_scale=scales[:, P * t : P * (t + 1)],
                     rhs=xg_w[:].bitcast(E4M3), rhs_scale=xg_s[:], start=True, stop=True,
                 )
 
-        def empty(copy, sb, ps, u):
-            copy(sb[u][:, : 2 * J], ps[u][:])
+        def empty(copy, sb, ps, t):
+            copy(sb[t][:, :J], ps[t][:])
 
         def look(copy, dst, sb, offsets, t):
-            u, v = divmod(t, 2)
-            copy(dst[u][:, v * O : (v + 1) * O], sb[u][:, v * J : (v + 2) * J].indirect(offsets[:]))
+            copy(dst[:, t * O : (t + 1) * O], sb[t][:].indirect(offsets[:]))
 
-        def larger(u):
-            nc.vector.tensor_tensor(ca[:, 2 * u * O : 2 * (u + 1) * O], a_g[u][:], b_g[u][:], ALU.max)
+        def larger(t0, t1):
+            cols = slice(t0 * O, t1 * O)
+            nc.vector.tensor_tensor(ca[:, cols], a_g[:, cols], b_g[:, cols], ALU.max)
 
         def neighbour(copy, t, h):
             copy(c_g[h][:, t * HALF : (t + 1) * HALF], ca[:, t * O : (t + 1) * O].indirect(idx4[:, h * 8 : (h + 1) * 8]))
 
-        def subtract(h):
+        def subtract(h, t0, t1):
             nc.vector.tensor_tensor(
-                diff[h][:].rearrange("p (t o) -> p t o", t=PACK),
-                ca[:].rearrange("p (t o) -> p t o", t=PACK)[:, :, h * HALF : (h + 1) * HALF],
-                c_g[h][:].rearrange("p (t o) -> p t o", t=PACK),
+                diff[h][:].rearrange("p (t o) -> p t o", t=PACK)[:, t0:t1, :],
+                ca[:].rearrange("p (t o) -> p t o", t=PACK)[:, t0:t1, h * HALF : (h + 1) * HALF],
+                c_g[h][:].rearrange("p (t o) -> p t o", t=PACK)[:, t0:t1, :],
                 ALU.subtract,
             )
 
@@ -159,15 +158,16 @@ def tile_list_pairedplaces_twow_further_plain_kernel(
 
         def short_way(h, g):
             rows, cols = slice(g * P, (g + 1) * P), slice(h * HALF, (h + 1) * HALF)
+            y_ps[h, g] = psum.tile([P, HALF], F32, name="y_ps%d%d" % (h, g), tag="bank_b%d" % (2 * h + g))
             nc.tensor.matmul_mx(
-                out=y_ps[h][g][:], lhsT=ws_w[:, rows].bitcast(E5M2), lhsT_scale=ws_s[:, rows],
+                out=y_ps[h, g][:], lhsT=ws_w[:, rows].bitcast(E5M2), lhsT_scale=ws_s[:, rows],
                 rhs=x5_w[:, cols].bitcast(E4M3), rhs_scale=x5_s[:, cols], start=True, stop=False,
             )
 
         def second_stage(h, g):
             rows = slice(g * P, (g + 1) * P)
             nc.tensor.matmul_mx(
-                out=y_ps[h][g][:], lhsT=wb_w[:, rows].bitcast(E5M2), lhsT_scale=wb_s[:, rows],
+                out=y_ps[h, g][:], lhsT=wb_w[:, rows].bitcast(E5M2), lhsT_scale=wb_s[:, rows],
                 rhs=hq_w[h][:].bitcast(E4M3), rhs_scale=hq_s[h][:], start=False, stop=True,
             )
 
@@ -177,46 +177,51 @@ def tile_list_pairedplaces_twow_further_plain_kernel(
         on_vector(xg_s[:], xt_s[:].indirect(idx[:]))
         on_vector(xg_w[:], xt_w[:].bitcast(U32).indirect(idx[:]))
         deal(nc.scalar.copy, w_w[:].bitcast(U16), w_raw[:].bitcast(U16))
-        deal(on_vector, w_s[:], w_s_raw[:])
+        deal(on_vector, w_s[:], w_s_raw[:], 0, 1)
+        deal(on_vector, w_s[:], w_s_raw[:], 1, PACK)
         deal(nc.scalar.copy, w2_w[:], w2_raw[:].bitcast(U32))
         first_stage(a_ps, w_w, 2, w_s, E2M1)
-        on_vector(x5_s[:], xt_s[:].indirect(idx5[:]))
-        on_vector(x5_w[:], xt_w[:].bitcast(U32).indirect(idx5[:]))
-        empty(on_vector, a_sb, a_ps, 0)
-        empty(nc.scalar.copy, a_sb, a_ps, 1)
         deal(on_vector, w2_s[:], w2_s_raw[:])
         first_stage(b_ps, w2_w, 1, w2_s, E5M2)
+        on_vector(x5_s[:], xt_s[:].indirect(idx5[:]))
+        x5_w = keep.tile([P, O], U32, name="x5_w", tag="w_s_then_x5", align_bytes=64)
+        on_vector(x5_w[:], xt_w[:].bitcast(U32).indirect(idx5[:]))
+        empty(on_vector, a_sb, a_ps, 0)
+        for t in (1, 2, 3):
+            empty(nc.scalar.copy, a_sb, a_ps, t)
         look(on_vector, a_g, a_sb, idx2, 0)
-        for t in (2, 3, 1):
-            look(on_scalar, a_g, a_sb, idx2, t)
+        look(on_vector, a_g, a_sb, idx2, 1)
+        look(on_scalar, a_g, a_sb, idx2, 2)
         empty(on_vector, b_sb, b_ps, 0)
-        empty(nc.scalar.copy, b_sb, b_ps, 1)
+        for t in (1, 2, 3):
+            empty(nc.scalar.copy, b_sb, b_ps, t)
         for h in range(2):
             for g in range(2):
                 short_way(h, g)
         look(on_vector, b_g, b_sb, idx3, 0)
         look(on_vector, b_g, b_sb, idx3, 1)
+        look(on_scalar, a_g, a_sb, idx2, 3)
         look(on_scalar, b_g, b_sb, idx3, 2)
         look(on_scalar, b_g, b_sb, idx3, 3)
-        larger(0)
-        larger(1)
-        neighbour(on_scalar, 0, 0)
+        larger(0, 2)
+        larger(2, 3)
+        neighbour(on_vector, 0, 0)
+        larger(3, 4)
         neighbour(on_scalar, 1, 0)
-        neighbour(on_vector, 2, 0)
-        neighbour(on_scalar, 3, 0)
-        subtract(0)
-        neighbour(on_scalar, 0, 1)
-        neighbour(on_scalar, 1, 1)
-        neighbour(on_vector, 2, 1)
-        neighbour(on_scalar, 3, 1)
+        neighbour(on_scalar, 2, 0)
+        neighbour(on_vector, 3, 0)
+        neighbour(on_vector, 3, 1)
+        subtract(0, 0, 4)
+        for t in (0, 1, 2):
+            neighbour(on_scalar, t, 1)
         magnitude(0)
-        subtract(1)
+        subtract(1, 0, 4)
         magnitude(1)
         for h in range(2):
             quantise(h)
             for g in range(2):
                 second_stage(h, g)
         for h in range(2):
-            on_vector(y_sb[h][:, 0, :], y_ps[h][0][:])
-            nc.scalar.copy(y_sb[h][:, 1, :], y_ps[h][1][:])
+            on_vector(y_sb[h][:, 0, :], y_ps[h, 0][:])
+            nc.scalar.copy(y_sb[h][:, 1, :], y_ps[h, 1][:])
             store(h)

@@ -21,12 +21,7 @@ P = 128
 PACK = 4
 HALF = O // 2
 LIST_COLS = J // 16
-WINDOW = 352
-
-
-def load_scale_rows(queue, plane, scales, quadrants):
-    for q in quadrants:
-        queue.dma_start(out=plane[32 * q : 32 * q + 4, :].bitcast(I32), in_=scales[0, 4 * q : 4 * q + 4, :].bitcast(I32))
+WINDOW = 353
 
 
 def load_scale_rows_filled(queue, plane, scales, quadrants):
@@ -52,9 +47,9 @@ def tile_list_pairedplaces_twow_further_plain_kernel(
         idx4 = lists.tile([P, LIST_COLS], U16, name="idx4")
         idx5 = lists.tile([P, LIST_COLS], U16, name="idx5")
 
-        xt_w = keep.tile([P, T], I32, name="xt_w", align_bytes=64)
+        xt_w = keep.tile([P, T], I32, name="xt_w", tag="xt_then_w2_s", align_bytes=64)
         xt_s = keep.tile([P, T], U8, name="xt_s", align_bytes=64)
-        w_raw = keep.tile([P, 2 * R], U8, name="w_raw", align_bytes=64)
+        w_raw = keep.tile([P, 2 * R], U8, name="w_raw", tag="w_then_w2", align_bytes=64)
         w2_raw = keep.tile([P, R], I32, name="w2_raw", align_bytes=64)
         w_s_raw = keep.tile([P, R], U8, name="w_s_raw", tag="w_s_then_x5", align_bytes=64)
         w2_s_raw = keep.tile([P, R], U8, name="w2_s_raw", align_bytes=64)
@@ -65,35 +60,32 @@ def tile_list_pairedplaces_twow_further_plain_kernel(
         a_sb = [keep.tile([P, WINDOW], F32, name="a_sb%d" % t) for t in range(PACK)]
         b_sb = [keep.tile([P, WINDOW], F32, name="b_sb%d" % t) for t in range(PACK)]
 
-        for plane in (ws_s, wb_s):
-            nc.vector.memset(plane[:].bitcast(I32), 0)
         for t in a_sb + b_sb:
             nc.vector.memset(t[:, J:], 0.0)
 
+        load_scale_rows_filled(nc.gpsimd, w2_s_raw, w2_scales, range(2, 3))
         nc.gpsimd.dma_start(out=w2_raw[:], in_=w2_words[0].rearrange("p c r -> p (c r)").bitcast(I32))
-        load_scale_rows_filled(nc.gpsimd, w2_s_raw, w2_scales, range(2, 4))
+        load_scale_rows_filled(nc.gpsimd, w2_s_raw, w2_scales, range(3, 4))
         nc.sync.dma_start(idx[:], offs)
         load_scale_rows_filled(nc.sync, xt_s, xt_scales, range(4))
+        nc.sync.dma_start(idx5[:], offs5)
         nc.sync.dma_start(out=xt_w[:], in_=xt_words[0].rearrange("p c r -> p (c r)").bitcast(I32))
         nc.sync.dma_start(out=w_raw[:].bitcast(I32), in_=w_words[0].bitcast(I32))
-        nc.sync.dma_start(idx5[:], offs5)
         load_scale_rows_filled(nc.sync, w_s_raw, w_scales, range(4))
         load_scale_rows_filled(nc.sync, w2_s_raw, w2_scales, range(2))
         nc.sync.dma_start(idx2[:], offs2)
         nc.sync.dma_start(idx3[:], offs3)
         nc.sync.dma_start(idx4[:], offs4)
         nc.sync.dma_start(out=ws_w[:], in_=ws_words[0].rearrange("p c r -> p (c r)").bitcast(I32))
-        load_scale_rows(nc.sync, ws_s, ws_scales, range(4))
+        load_scale_rows_filled(nc.sync, ws_s, ws_scales, range(4))
         nc.sync.dma_start(out=wb_w[:], in_=wb_words[0].rearrange("p c r -> p (c r)").bitcast(I32))
-        load_scale_rows(nc.sync, wb_s, wb_scales, range(4))
+        load_scale_rows_filled(nc.sync, wb_s, wb_scales, range(4))
 
         xg_s = keep.tile([P, J], U8, name="xg_s", align_bytes=64)
         xg_w = keep.tile([P, J], U32, name="xg_w", align_bytes=64)
         x5_s = keep.tile([P, O], U8, name="x5_s", align_bytes=64)
         w_w = keep.tile([P, 2 * R], U8, name="w_w", align_bytes=64)
-        w2_w = keep.tile([P, R], U32, name="w2_w", align_bytes=64)
         w_s = keep.tile([P, R], U8, name="w_s", align_bytes=64)
-        w2_s = keep.tile([P, R], U8, name="w2_s", align_bytes=64)
         a_ps = [psum.tile([P, J], F32, name="a_ps%d" % t) for t in range(PACK)]
         b_ps = [psum.tile([P, J], F32, name="b_ps%d" % t, tag="bank_b%d" % t) for t in range(PACK)]
         y_ps = {}
@@ -106,7 +98,6 @@ def tile_list_pairedplaces_twow_further_plain_kernel(
         hq_w = [keep.tile([P, HALF], U32, name="hq_w%d" % h, align_bytes=64) for h in range(2)]
         hq_s = [keep.tile([P, HALF], U8, name="hq_s%d" % h, align_bytes=64) for h in range(2)]
         y_sb = [keep.tile([P, 2, HALF], F32, name="y_sb%d" % h) for h in range(2)]
-        out_v = out.rearrange("(g p) o -> p g o", p=P)
 
         def on_vector(dst, src):
             nc.vector.tensor_copy(dst, src)
@@ -171,21 +162,24 @@ def tile_list_pairedplaces_twow_further_plain_kernel(
                 rhs=hq_w[h][:].bitcast(E4M3), rhs_scale=hq_s[h][:], start=False, stop=True,
             )
 
-        def store(h):
-            nc.sync.dma_start(out=out_v[:, :, h * HALF : (h + 1) * HALF], in_=y_sb[h][:])
+        def store(queue, h, g):
+            queue.dma_start(out=out[g * P : (g + 1) * P, h * HALF : (h + 1) * HALF], in_=y_sb[h][:, g, :])
 
         on_vector(xg_s[:], xt_s[:].indirect(idx[:]))
         on_vector(xg_w[:], xt_w[:].bitcast(U32).indirect(idx[:]))
-        deal(nc.scalar.copy, w_w[:].bitcast(U16), w_raw[:].bitcast(U16))
+        deal(nc.scalar.copy, w_w[:].bitcast(U16), w_raw[:].bitcast(U16), 0, 1)
+        deal(nc.scalar.copy, w_w[:].bitcast(U16), w_raw[:].bitcast(U16), 1, PACK)
         deal(on_vector, w_s[:], w_s_raw[:], 0, 1)
         deal(on_vector, w_s[:], w_s_raw[:], 1, PACK)
+        w2_w = keep.tile([P, R], U32, name="w2_w", tag="w_then_w2", align_bytes=64)
         deal(nc.scalar.copy, w2_w[:], w2_raw[:].bitcast(U32))
         first_stage(a_ps, w_w, 2, w_s, E2M1)
-        deal(on_vector, w2_s[:], w2_s_raw[:])
-        first_stage(b_ps, w2_w, 1, w2_s, E5M2)
         on_vector(x5_s[:], xt_s[:].indirect(idx5[:]))
         x5_w = keep.tile([P, O], U32, name="x5_w", tag="w_s_then_x5", align_bytes=64)
         on_vector(x5_w[:], xt_w[:].bitcast(U32).indirect(idx5[:]))
+        w2_s = keep.tile([P, R], U8, name="w2_s", tag="xt_then_w2_s", align_bytes=64)
+        deal(on_vector, w2_s[:], w2_s_raw[:])
+        first_stage(b_ps, w2_w, 1, w2_s, E5M2)
         empty(on_vector, a_sb, a_ps, 0)
         for t in (1, 2, 3):
             empty(nc.scalar.copy, a_sb, a_ps, t)
@@ -224,4 +218,5 @@ def tile_list_pairedplaces_twow_further_plain_kernel(
         for h in range(2):
             on_vector(y_sb[h][:, 0, :], y_ps[h, 0][:])
             nc.scalar.copy(y_sb[h][:, 1, :], y_ps[h, 1][:])
-            store(h)
+            store(nc.sync, h, 0)
+            store(nc.sync if h == 0 else nc.scalar, h, 1)

@@ -180,37 +180,28 @@ def tile_list_pairedplaces_twow_further_plain_kernel(
         w2_s = keep.tile([P, R], U8, name="w2_s", tag="xt_then_w2_s", align_bytes=64)
         deal(on_vector, w2_s[:], w2_s_raw[:])
         first_stage(b_ps, w2_w, 1, w2_s, E5M2)
-        empty(on_vector, a_sb, a_ps, 0)
-        for t in (1, 2, 3):
-            empty(nc.scalar.copy, a_sb, a_ps, t)
-        look(on_vector, a_g, a_sb, idx2, 0)
-        look(on_vector, a_g, a_sb, idx2, 1)
-        look(on_scalar, a_g, a_sb, idx2, 2)
-        empty(on_vector, b_sb, b_ps, 0)
-        for t in (1, 2, 3):
-            empty(nc.scalar.copy, b_sb, b_ps, t)
+        for sb, ps, dst, offsets in ((a_sb, a_ps, a_g, idx2), (b_sb, b_ps, b_g, idx3)):
+            for t in (0, 1):
+                empty(on_vector, sb, ps, t)
+            for t in (2, 3):
+                empty(nc.scalar.copy, sb, ps, t)
+            for t in (0, 1):
+                look(on_vector, dst, sb, offsets, t)
+            for t in (2, 3):
+                look(on_scalar, dst, sb, offsets, t)
         for h in range(2):
             for g in range(2):
                 short_way(h, g)
-        look(on_vector, b_g, b_sb, idx3, 0)
-        look(on_vector, b_g, b_sb, idx3, 1)
-        look(on_scalar, a_g, a_sb, idx2, 3)
-        look(on_scalar, b_g, b_sb, idx3, 2)
-        look(on_scalar, b_g, b_sb, idx3, 3)
-        larger(0, 2)
-        larger(2, 3)
-        neighbour(on_vector, 0, 0)
-        larger(3, 4)
-        neighbour(on_scalar, 1, 0)
-        neighbour(on_scalar, 2, 0)
-        neighbour(on_vector, 3, 0)
-        neighbour(on_vector, 3, 1)
-        subtract(0, 0, 4)
-        for t in (0, 1, 2):
-            neighbour(on_scalar, t, 1)
-        magnitude(0)
-        subtract(1, 0, 4)
-        magnitude(1)
+        larger(0, 1)
+        larger(1, 2)
+        larger(2, 4)
+        for t, h in ((0, 0), (1, 0), (0, 1), (2, 0), (1, 1), (2, 1)):
+            neighbour(on_scalar, t, h)
+        for h in range(2):
+            neighbour(on_vector, 3, h)
+        for h in range(2):
+            subtract(h, 0, 4)
+            magnitude(h)
         for h in range(2):
             quantise(h)
             for g in range(2):

from contextlib import ExitStack

import concourse.mybir as mybir

K, T, J, R, O, N = 512, 1024, 256, 512, 256, 256
FLOPS = 2 * (2 * K * R * J + R * N * O + K * N * O)

F32 = mybir.dt.float32
BF16 = mybir.dt.bfloat16
I32 = mybir.dt.int32
U32 = mybir.dt.uint32
U16 = mybir.dt.uint16
U8 = mybir.dt.uint8
E4M3 = mybir.dt.float8_e4m3fn_x4
E5M2 = mybir.dt.float8_e5m2_x4
E2M1 = mybir.dt.float4_e2m1fn_x4
ACT = mybir.ActivationFunctionType
ALU = mybir.AluOpType

P = 128
PACK = 4
HALF = O // 2
LIST_COLS = J // 16
WINDOW = 353


def load_scale_rows_filled(queue, plane, scales, quadrants):
    width = scales.shape[2] // 4
    for q in quadrants:
        rows = scales[0, 4 * q : 4 * q + 4, :].bitcast(I32).rearrange("(o r) w -> o r w", o=1)
        queue.dma_start(out=plane[32 * q : 32 * q + 32, :].bitcast(I32), in_=rows.to_broadcast([8, 4, width]))


def tile_list_pairedplaces_twow_further_plain_kernel(
    tc, xt_words, xt_scales, w_words, w_scales, w2_words, w2_scales, wb_words, wb_scales, ws_words, ws_scales,
    offs, offs2, offs3, offs4, offs5, out,
):
    nc = tc.nc
    with ExitStack() as ctx:
        lists = ctx.enter_context(tc.tile_pool(name="lists", bufs=1))
        keep = ctx.enter_context(tc.tile_pool(name="keep", bufs=1))
        psum = ctx.enter_context(tc.psum_pool(name="psum", bufs=1))

        idx = lists.tile([P, LIST_COLS], U16, name="idx")
        idx2 = lists.tile([P, LIST_COLS], U16, name="idx2")
        idx3 = lists.tile([P, LIST_COLS], U16, name="idx3")
        idx4 = lists.tile([P, LIST_COLS], U16, name="idx4")
        idx5 = lists.tile([P, LIST_COLS], U16, name="idx5")

        xt_w = keep.tile([P, T], I32, name="xt_w", tag="xt_then_w2_s", align_bytes=64)
        xt_s = keep.tile([P, T], U8, name="xt_s", align_bytes=64)
        w_raw = keep.tile([P, 2 * R], U8, name="w_raw", tag="w_then_w2", align_bytes=64)
        w2_raw = keep.tile([P, R], I32, name="w2_raw", align_bytes=64)
        w_s_raw = keep.tile([P, R], U8, name="w_s_raw", tag="w_s_then_x5", align_bytes=64)
        w2_s_raw = keep.tile([P, R], U8, name="w2_s_raw", align_bytes=64)
        wb_w = keep.tile([P, N], I32, name="wb_w", align_bytes=64)
        ws_w = keep.tile([P, N], I32, name="ws_w", align_bytes=64)
        wb_s = keep.tile([P, N], U8, name="wb_s", align_bytes=64)
        ws_s = keep.tile([P, N], U8, name="ws_s", align_bytes=64)
        a_sb = [keep.tile([P, WINDOW], F32, name="a_sb%d" % t) for t in range(PACK)]
        b_sb = [keep.tile([P, WINDOW], F32, name="b_sb%d" % t) for t in range(PACK)]

        for t in a_sb + b_sb:
            nc.vector.memset(t[:, J:], 0.0)

        load_scale_rows_filled(nc.gpsimd, w2_s_raw, w2_scales, range(2, 3))
        nc.gpsimd.dma_start(out=w2_raw[:], in_=w2_words[0].rearrange("p c r -> p (c r)").bitcast(I32))
        load_scale_rows_filled(nc.gpsimd, w2_s_raw, w2_scales, range(3, 4))
        nc.sync.dma_start(idx[:], offs)
        load_scale_rows_filled(nc.sync, xt_s, xt_scales, range(4))
        nc.sync.dma_start(idx5[:], offs5)
        nc.sync.dma_start(out=xt_w[:], in_=xt_words[0].rearrange("p c r -> p (c r)").bitcast(I32))
        nc.sync.dma_start(out=w_raw[:].bitcast(I32), in_=w_words[0].bitcast(I32))
        load_scale_rows_filled(nc.sync, w_s_raw, w_scales, range(4))
        load_scale_rows_filled(nc.sync, w2_s_raw, w2_scales, range(2))
        nc.sync.dma_start(idx2[:], offs2)
        nc.sync.dma_start(idx3[:], offs3)
        nc.sync.dma_start(idx4[:], offs4)
        nc.sync.dma_start(out=ws_w[:], in_=ws_words[0].rearrange("p c r -> p (c r)").bitcast(I32))
        load_scale_rows_filled(nc.sync, ws_s, ws_scales, range(4))
        nc.sync.dma_start(out=wb_w[:], in_=wb_words[0].rearrange("p c r -> p (c r)").bitcast(I32))
        load_scale_rows_filled(nc.sync, wb_s, wb_scales, range(4))

        xg_s = keep.tile([P, J], U8, name="xg_s", align_bytes=64)
        xg_w = keep.tile([P, J], U32, name="xg_w", align_bytes=64)
        x5_s = keep.tile([P, O], U8, name="x5_s", align_bytes=64)
        w_w = keep.tile([P, 2 * R], U8, name="w_w", align_bytes=64)
        w_s = keep.tile([P, R], U8, name="w_s", align_bytes=64)
        a_ps = [psum.tile([P, J], F32, name="a_ps%d" % t) for t in range(PACK)]
        b_ps = [psum.tile([P, J], F32, name="b_ps%d" % t, tag="bank_b%d" % t) for t in range(PACK)]
        y_ps = {}
        a_g = keep.tile([P, PACK * O], F32, name="a_g")
        b_g = keep.tile([P, PACK * O], F32, name="b_g")
        ca = keep.tile([P, PACK * O], F32, name="ca")
        c_g = [keep.tile([P, PACK * HALF], F32, name="c_g%d" % h) for h in range(2)]
        diff = [keep.tile([P, PACK * HALF], F32, name="diff%d" % h) for h in range(2)]
        hid = [keep.tile([P, HALF * PACK], BF16, name="hid%d" % h, align_bytes=64) for h in range(2)]
        hq_w = [keep.tile([P, HALF], U32, name="hq_w%d" % h, align_bytes=64) for h in range(2)]
        hq_s = [keep.tile([P, HALF], U8, name="hq_s%d" % h, align_bytes=64) for h in range(2)]
        y_sb = [keep.tile([P, 2, HALF], F32, name="y_sb%d" % h) for h in range(2)]

        def on_vector(dst, src):
            nc.vector.tensor_copy(dst, src)

        def on_scalar(dst, src):
            nc.scalar.activation(dst, src, ACT.Copy)

        def deal(copy, dst, src, t0=0, t1=PACK):
            copy(dst.rearrange("p (t m) -> p m t", t=PACK)[:, :, t0:t1], src.rearrange("p (m t) -> p m t", t=PACK)[:, :, t0:t1])

        def first_stage(ps, words, width, scales, fmt):
            for t in range(PACK):
                nc.tensor.matmul_mx(
                    out=ps[t][:],
                    lhsT=words[:, width * P * t : width * P * (t + 1)].bitcast(fmt), lhsT_scale=scales[:, P * t : P * (t + 1)],
                    rhs=xg_w[:].bitcast(E4M3), rhs_scale=xg_s[:], start=True, stop=True,
                )

        def empty(copy, sb, ps, t):
            copy(sb[t][:, :J], ps[t][:])

        def look(copy, dst, sb, offsets, t):
            copy(dst[:, t * O : (t + 1) * O], sb[t][:].indirect(offsets[:]))

        def larger(t0, t1):
            cols = slice(t0 * O, t1 * O)
            nc.vector.tensor_tensor(ca[:, cols], a_g[:, cols], b_g[:, cols], ALU.max)

        def neighbour(copy, t, h):
            copy(c_g[h][:, t * HALF : (t + 1) * HALF], ca[:, t * O : (t + 1) * O].indirect(idx4[:, h * 8 : (h + 1) * 8]))

        def subtract(h, t0, t1):
            nc.vector.tensor_tensor(
                diff[h][:].rearrange("p (t o) -> p t o", t=PACK)[:, t0:t1, :],
                ca[:].rearrange("p (t o) -> p t o", t=PACK)[:, t0:t1, h * HALF : (h + 1) * HALF],
                c_g[h][:].rearrange("p (t o) -> p t o", t=PACK)[:, t0:t1, :],
                ALU.subtract,
            )

        def magnitude(h):
            nc.scalar.activation(
                hid[h][:].rearrange("p (c i t) -> p c t i", i=4, t=PACK),
                diff[h][:].rearrange("p (t c i) -> p c t i", i=4, t=PACK),
                ACT.Abs,
            )

        def quantise(h):
            nc.vector.quantize_mx(out=hq_w[h][:].bitcast(E4M3), scales=hq_s[h][:], in_=hid[h][:])

        def short_way(h, g):
            rows, cols = slice(g * P, (g + 1) * P), slice(h * HALF, (h + 1) * HALF)
            y_ps[h, g] = psum.tile([P, HALF], F32, name="y_ps%d%d" % (h, g), tag="bank_b%d" % (2 * h + g))
            nc.tensor.matmul_mx(
                out=y_ps[h, g][:], lhsT=ws_w[:, rows].bitcast(E5M2), lhsT_scale=ws_s[:, rows],
                rhs=x5_w[:, cols].bitcast(E4M3), rhs_scale=x5_s[:, cols], start=True, stop=False,
            )

        def second_stage(h, g):
            rows = slice(g * P, (g + 1) * P)
            nc.tensor.matmul_mx(
                out=y_ps[h, g][:], lhsT=wb_w[:, rows].bitcast(E5M2), lhsT_scale=wb_s[:, rows],
                rhs=hq_w[h][:].bitcast(E4M3), rhs_scale=hq_s[h][:], start=False, stop=True,
            )

        def store(queue, h, g):
            queue.dma_start(out=out[g * P : (g + 1) * P, h * HALF : (h + 1) * HALF], in_=y_sb[h][:, g, :])

        on_vector(xg_s[:], xt_s[:].indirect(idx[:]))
        on_vector(xg_w[:], xt_w[:].bitcast(U32).indirect(idx[:]))
        deal(nc.scalar.copy, w_w[:].bitcast(U16), w_raw[:].bitcast(U16), 0, 1)
        deal(nc.scalar.copy, w_w[:].bitcast(U16), w_raw[:].bitcast(U16), 1, PACK)
        deal(on_vector, w_s[:], w_s_raw[:], 0, 1)
        deal(on_vector, w_s[:], w_s_raw[:], 1, PACK)
        w2_w = keep.tile([P, R], U32, name="w2_w", tag="w_then_w2", align_bytes=64)
        deal(nc.scalar.copy, w2_w[:], w2_raw[:].bitcast(U32))
        first_stage(a_ps, w_w, 2, w_s, E2M1)
        on_vector(x5_s[:], xt_s[:].indirect(idx5[:]))
        x5_w = keep.tile([P, O], U32, name="x5_w", tag="w_s_then_x5", align_bytes=64)
        on_vector(x5_w[:], xt_w[:].bitcast(U32).indirect(idx5[:]))
        w2_s = keep.tile([P, R], U8, name="w2_s", tag="xt_then_w2_s", align_bytes=64)
        deal(on_vector, w2_s[:], w2_s_raw[:])
        first_stage(b_ps, w2_w, 1, w2_s, E5M2)
        for sb, ps, dst, offsets in ((a_sb, a_ps, a_g, idx2), (b_sb, b_ps, b_g, idx3)):
            for t in (0, 1):
                empty(on_vector, sb, ps, t)
            for t in (2, 3):
                empty(nc.scalar.copy, sb, ps, t)
            for t in (0, 1):
                look(on_vector, dst, sb, offsets, t)
            for t in (2, 3):
                look(on_scalar, dst, sb, offsets, t)
        for h in range(2):
            for g in range(2):
                short_way(h, g)
        larger(0, 1)
        larger(1, 2)
        larger(2, 4)
        for t, h in ((0, 0), (1, 0), (0, 1), (2, 0), (1, 1), (2, 1)):
            neighbour(on_scalar, t, h)
        for h in range(2):
            neighbour(on_vector, 3, h)
        for h in range(2):
            subtract(h, 0, 4)
            magnitude(h)
        for h in range(2):
            quantise(h)
            for g in range(2):
                second_stage(h, g)
        for h in range(2):
            on_vector(y_sb[h][:, 0, :], y_ps[h, 0][:])
            nc.scalar.copy(y_sb[h][:, 1, :], y_ps[h, 1][:])
            store(nc.sync, h, 0)
            store(nc.sync if h == 0 else nc.scalar, h, 1)
